import numpy as np
import ml_dtypes


def mxq(x, axis, fmt="e4m3"):
    dtype, down = {"e4m3": (ml_dtypes.float8_e4m3fn, 7), "e5m2": (ml_dtypes.float8_e5m2, 14)}[fmt]
    v = np.moveaxis(np.asarray(x, np.float32).astype(ml_dtypes.bfloat16).astype(np.float64), axis, -1)
    blocks = v.reshape(v.shape[:-1] + (-1, 32))
    amax = np.abs(blocks).max(-1, keepdims=True)
    byte = np.maximum(np.where(amax > 0, np.frexp(amax)[1] - 1 + 127, 0) - down, 1)
    scale = np.exp2(byte - 127.0)
    codes = (blocks / scale).astype(np.float32).astype(dtype).astype(np.float64)
    return np.moveaxis((codes * scale).reshape(v.shape), -1, axis)


WIDE = False


def mx_kscale(k):
    if not WIDE:
        return np.ones(k)
    levels = np.array([10, -10, 5, -5, 0])
    if k % 512:
        return np.exp2(np.random.permutation(np.resize(levels, k // 32))).repeat(32)
    a = np.empty((k // 512, 16))
    for p in range(k // 512):
        a[p, :8] = np.random.permutation(np.resize(levels, 8))
        for g in range(8):
            far = levels[np.abs(levels - a[p, g]) >= 10]
            a[p, g + 8] = far[np.random.randint(len(far))]
    return np.exp2(a.ravel()).repeat(32)


def f64(x):
    return np.asarray(x).astype(np.float64)


def striped(idx):
    return np.tile(idx.reshape(-1, 16).T, (8, 1)).astype(np.uint16)


def unstriped(offs):
    return offs[:16].T.reshape(-1).astype(np.int64)


def pack_weight(w):
    k, n = w.shape
    w = f64(np.asarray(w, np.float32).astype(ml_dtypes.bfloat16)).reshape(k // 32, 32, n)
    amax = np.abs(w).max(1)
    byte = np.clip(np.where(amax > 0, np.frexp(amax)[1] - 1 + 127 - 7, 1), 1, 254)
    scaled = (w * np.exp2(127.0 - byte)[:, None, :]).reshape(k, n).astype(np.float32)
    words = np.ascontiguousarray(scaled.reshape(k // 512, 128, 4, n).transpose(0, 1, 3, 2)).astype(ml_dtypes.float8_e4m3fn).view(np.uint8)
    return words, np.ascontiguousarray(byte.astype(np.uint8).reshape(k // 512, 16, n))


def unpack_weight(words, scales):
    g, p, n, _ = words.shape
    vals = np.ascontiguousarray(words).view(ml_dtypes.float8_e4m3fn).astype(np.float64) * np.repeat(np.exp2(scales.astype(np.float64) - 127.0), 8, axis=1)[..., None]
    return vals.transpose(0, 1, 3, 2).reshape(g * 512, n)


K, T, N = 1024, 512, 128
P = 2 ** 7


def setup_inputs():
    n = np.random.standard_normal
    s = mx_kscale(K)[:, None]
    packed_xT = pack_weight(n((K, T)) * s)
    return {
        "x_words": packed_xT[0],
        "x_scales": packed_xT[1],
        "w1": (n((K, N)) / np.sqrt(K) / s).astype(np.float32),
        "frac": np.tile(np.random.uniform(0.05, 0.95, T), (P, 1)).astype(np.float32),
        "left": striped(np.random.permutation(T)),
        "right": striped(np.random.permutation(T)),
    }


def reference(x_words, x_scales, w1, frac, left, right):
    xq = unpack_weight(x_words, x_scales)
    y = mxq(f64(w1), 0, "e4m3").T @ xq
    l = y[:, unstriped(left)]
    return l + (y[:, unstriped(right)] - l) * f64(frac)[:1]

@@ -1,0 +1,150 @@
+from contextlib import ExitStack
+
+import concourse.mybir as mybir
+
+K, T, N = 1024, 512, 128
+FLOPS = 2 * K * T * N
+
+F32 = mybir.dt.float32
+BF16 = mybir.dt.bfloat16
+I32 = mybir.dt.int32
+U32 = mybir.dt.uint32
+U16 = mybir.dt.uint16
+U8 = mybir.dt.uint8
+FP8X4 = mybir.dt.float8_e4m3fn_x4
+MULT = mybir.AluOpType.mult
+ADD = mybir.AluOpType.add
+COPY = mybir.ActivationFunctionType.Copy
+
+P = 128
+PACK = 4
+PASSES = 2
+GROUPS = ((0, 256), (256, 384), (384, 512))
+XPIECES = ((0, 0, 512), (1, 0, 512))
+
+
+def tile_picked_wlerp_none_l_kernel(tc, x_words, x_scales, w1, frac, left, right, out):
+    nc = tc.nc
+    with ExitStack() as ctx:
+        keep = ctx.enter_context(tc.tile_pool(name="keep", bufs=1))
+        psum = ctx.enter_context(tc.psum_pool(name="psum", bufs=1))
+
+        w_rows = w1.rearrange("(z p j) m -> z p (j m)", z=PASSES, j=PACK)
+        w_raw = [keep.tile([P, PACK * N], F32, name="w_raw%d" % z) for z in range(PASSES)]
+        x_plane = keep.tile([P, PASSES, T], U8, name="x_plane", align_bytes=64)
+        words = [x_words[z].rearrange("p n t -> p (n t)").bitcast(I32) for z in range(PASSES)]
+        x_tiles = [keep.tile([P, b - a], U32, name="x%d_%d" % (z, a), align_bytes=64) for z, a, b in XPIECES]
+        f_right = keep.tile([P, T], F32, name="f_right")
+        right_offs = keep.tile([P, T // 16], U16, name="right_offs")
+        left_offs = keep.tile([P, T // 16], U16, name="left_offs")
+
+        def load_w(z, eng):
+            eng.dma_start(out=w_raw[z][:], in_=w_rows[z])
+
+        def load_s(q, eng):
+            eng.dma_start(
+                out=x_plane[32 * q : 32 * q + 4, :, :].bitcast(I32),
+                in_=x_scales[:, 4 * q : 4 * q + 4, :].rearrange("z r c -> r z c").bitcast(I32),
+            )
+
+        def load_x(i, eng):
+            z, a, b = XPIECES[i]
+            eng.dma_start(out=x_tiles[i][:].bitcast(I32), in_=words[z][:, a:b])
+
+        def load_f(eng):
+            eng.dma_start(out=f_right[:], in_=frac)
+
+        load_w(0, nc.sync)
+        load_w(1, nc.sync)
+        for q in range(4):
+            load_s(q, nc.scalar)
+        load_x(0, nc.sync)
+        load_x(1, nc.sync)
+        load_f(nc.sync)
+        nc.sync.dma_start(right_offs[:], right)
+        nc.sync.dma_start(left_offs[:], left)
+
+        w_codes = []
+        w_plane = []
+        grouped = []
+        for z in range(PASSES):
+            grouped.append(keep.tile([P, N, PACK], BF16, name="grouped%d" % z, align_bytes=64))
+            w_codes.append(keep.tile([P, N], U32, name="w_codes%d" % z, align_bytes=64))
+            w_plane.append(keep.tile([P, N], U8, name="w_plane%d" % z, align_bytes=64))
+
+        def cast(z, a, b, on_scalar):
+            dst = grouped[z][:, a:b, :].rearrange("p (c i) t -> p c t i", i=4)
+            src = w_raw[z][:].rearrange("p (t c i) -> p c t i", t=PACK, i=4)[:, a // 4 : b // 4, :, :]
+            if on_scalar:
+                nc.scalar.copy(out=dst, in_=src)
+            else:
+                nc.vector.tensor_copy(out=dst, in_=src)
+
+        def quant(z):
+            nc.vector.quantize_mx(
+                out=w_codes[z][:].bitcast(FP8X4), scales=w_plane[z][:], in_=grouped[z][:].rearrange("p m t -> p (m t)")
+            )
+
+        cast(0, 0, N, False)
+        quant(0)
+        cast(1, 0, N, False)
+        quant(1)
+
+        banks = [psum.tile([P, b - a], F32, name="bank%d" % i) for i, (a, b) in enumerate(GROUPS)]
+        for z in range(PASSES):
+            for i, (a, b) in enumerate(GROUPS):
+                j = [n for n, (pz, pa, pb) in enumerate(XPIECES) if pz == z and pa <= a and b <= pb][0]
+                base = XPIECES[j][1]
+                nc.tensor.matmul_mx(
+                    out=banks[i][:],
+                    lhsT=w_codes[z][:].bitcast(FP8X4),
+                    lhsT_scale=w_plane[z][:],
+                    rhs=x_tiles[j][:, a - base : b - base].bitcast(FP8X4),
+                    rhs_scale=x_plane[:, z, a:b],
+                    start=(z == 0),
+                    stop=(z == PASSES - 1),
+                )
+
+        y = keep.tile([P, T], F32, name="y")
+
+        def drain(i, on_scalar):
+            a, b = GROUPS[i]
+            if on_scalar:
+                nc.scalar.copy(out=y[:, a:b], in_=banks[i][:])
+            else:
+                nc.vector.tensor_copy(out=y[:, a:b], in_=banks[i][:])
+
+        drain(0, False)
+        drain(1, True)
+        drain(2, True)
+
+        f_left = keep.tile([P, T], F32, name="f_left")
+        r = keep.tile([P, T], F32, name="r")
+        l = keep.tile([P, T], F32, name="l")
+        o = keep.tile([P, T], F32, name="o")
+
+        def comp(a, b):
+            nc.scalar.activation(out=f_left[:, a:b], in_=f_right[:, a:b], func=COPY, scale=-1.0, bias=1.0)
+
+        def gr(a, b):
+            nc.vector.tensor_tensor(r[:, a:b], y[:].indirect(right_offs[:, a // 16 : b // 16]), f_right[:, a:b], MULT)
+
+        def gl(a, b):
+            nc.vector.tensor_tensor(l[:, a:b], y[:].indirect(left_offs[:, a // 16 : b // 16]), f_left[:, a:b], MULT)
+
+        def add(a, b):
+            nc.vector.tensor_tensor(o[:, a:b], r[:, a:b], l[:, a:b], ADD)
+
+        def store(a, b, eng):
+            eng.dma_start(out=out[:, a:b], in_=o[:, a:b])
+
+        comp(0, 256)
+        comp(256, 512)
+        gr(0, 256)
+        gl(0, 256)
+        gr(256, 512)
+        gl(256, 512)
+        add(0, 256)
+        store(0, 256, nc.scalar)
+        add(256, 512)
+        store(256, 512, nc.sync)

@@ -55,9 +55,11 @@ def tile_picked_wlerp_none_l_kernel(tc, x_words, x_scales, w1, frac, left, right
             eng.dma_start(out=f_right[:], in_=frac)
 
         load_w(0, nc.sync)
+        load_s(0, nc.scalar)
         load_w(1, nc.sync)
-        for q in range(4):
-            load_s(q, nc.scalar)
+        load_s(1, nc.scalar)
+        load_s(2, nc.sync)
+        load_s(3, nc.sync)
         load_x(0, nc.sync)
         load_x(1, nc.sync)
         load_f(nc.sync)

@@ -19,7 +19,7 @@ COPY = mybir.ActivationFunctionType.Copy
 P = 128
 PACK = 4
 PASSES = 2
-GROUPS = ((0, 256), (256, 384), (384, 512))
+GROUPS = ((0, 128), (128, 256), (256, 384), (384, 512))
 XPIECES = ((0, 0, 512), (1, 0, 512))
 
 
@@ -43,8 +43,8 @@ def tile_picked_wlerp_none_l_kernel(tc, x_words, x_scales, w1, frac, left, right
 
         def load_s(q, eng):
             eng.dma_start(
-                out=x_plane[32 * q : 32 * q + 4, :, :].bitcast(I32),
-                in_=x_scales[:, 4 * q : 4 * q + 4, :].rearrange("z r c -> r z c").bitcast(I32),
+                out=x_plane[q:P:32, :, :].bitcast(I32),
+                in_=x_scales[:, q:16:4, :].rearrange("z r c -> r z c").bitcast(I32),
             )
 
         def load_x(i, eng):
@@ -116,9 +116,8 @@ def tile_picked_wlerp_none_l_kernel(tc, x_words, x_scales, w1, frac, left, right
             else:
                 nc.vector.tensor_copy(out=y[:, a:b], in_=banks[i][:])
 
-        drain(0, False)
-        drain(1, True)
-        drain(2, True)
+        for i in range(4):
+            drain(i, False)
 
         f_left = keep.tile([P, T], F32, name="f_left")
         r = keep.tile([P, T], F32, name="r")
@@ -126,7 +125,7 @@ def tile_picked_wlerp_none_l_kernel(tc, x_words, x_scales, w1, frac, left, right
         o = keep.tile([P, T], F32, name="o")
 
         def comp(a, b):
-            nc.scalar.activation(out=f_left[:, a:b], in_=f_right[:, a:b], func=COPY, scale=-1.0, bias=1.0)
+            nc.vector.tensor_scalar(f_left[:, a:b], f_right[:, a:b], -1.0, 1.0, MULT, ADD)
 
         def gr(a, b):
             nc.vector.tensor_tensor(r[:, a:b], y[:].indirect(right_offs[:, a // 16 : b // 16]), f_right[:, a:b], MULT)
@@ -140,8 +139,7 @@ def tile_picked_wlerp_none_l_kernel(tc, x_words, x_scales, w1, frac, left, right
         def store(a, b, eng):
             eng.dma_start(out=out[:, a:b], in_=o[:, a:b])
 
-        comp(0, 256)
-        comp(256, 512)
+        comp(0, 512)
         gr(0, 256)
         gl(0, 256)
         gr(256, 512)

@@ -14,13 +14,17 @@ U8 = mybir.dt.uint8
 FP8X4 = mybir.dt.float8_e4m3fn_x4
 MULT = mybir.AluOpType.mult
 ADD = mybir.AluOpType.add
-COPY = mybir.ActivationFunctionType.Copy
 
 P = 128
 PACK = 4
-PASSES = 2
-GROUPS = ((0, 128), (128, 256), (256, 384), (384, 512))
-XPIECES = ((0, 0, 512), (1, 0, 512))
+PASSES = K // (P * PACK)
+QUADRANT = 32
+SCALE_ROWS = 4
+STRIPE = 16
+RUN = 4
+BANK_COLS = 128
+HALF = T // 2
+SPARE = 16
 
 
 def tile_picked_wlerp_none_l_kernel(tc, x_words, x_scales, w1, frac, left, right, out):
@@ -29,122 +33,82 @@ def tile_picked_wlerp_none_l_kernel(tc, x_words, x_scales, w1, frac, left, right
         keep = ctx.enter_context(tc.tile_pool(name="keep", bufs=1))
         psum = ctx.enter_context(tc.psum_pool(name="psum", bufs=1))
 
-        w_rows = w1.rearrange("(z p j) m -> z p (j m)", z=PASSES, j=PACK)
         w_raw = [keep.tile([P, PACK * N], F32, name="w_raw%d" % z) for z in range(PASSES)]
         x_plane = keep.tile([P, PASSES, T], U8, name="x_plane", align_bytes=64)
-        words = [x_words[z].rearrange("p n t -> p (n t)").bitcast(I32) for z in range(PASSES)]
-        x_tiles = [keep.tile([P, b - a], U32, name="x%d_%d" % (z, a), align_bytes=64) for z, a, b in XPIECES]
+        x_codes = [keep.tile([P, T], U32, name="x_codes%d" % z, align_bytes=64) for z in range(PASSES)]
         f_right = keep.tile([P, T], F32, name="f_right")
-        right_offs = keep.tile([P, T // 16], U16, name="right_offs")
-        left_offs = keep.tile([P, T // 16], U16, name="left_offs")
+        right_offs = keep.tile([P, T // STRIPE], U16, name="right_offs")
+        left_offs = keep.tile([P, T // STRIPE], U16, name="left_offs")
 
-        def load_w(z, eng):
-            eng.dma_start(out=w_raw[z][:], in_=w_rows[z])
+        w_rows = w1.rearrange("(z p t) m -> z p (t m)", z=PASSES, t=PACK)
 
-        def load_s(q, eng):
-            eng.dma_start(
-                out=x_plane[q:P:32, :, :].bitcast(I32),
-                in_=x_scales[:, q:16:4, :].rearrange("z r c -> r z c").bitcast(I32),
+        def load_scales(r, queue):
+            queue.dma_start(
+                out=x_plane[r:P:QUADRANT, :, :].bitcast(I32),
+                in_=x_scales[:, r : P // 8 : SCALE_ROWS, :].rearrange("z q c -> q z c").bitcast(I32),
             )
 
-        def load_x(i, eng):
-            z, a, b = XPIECES[i]
-            eng.dma_start(out=x_tiles[i][:].bitcast(I32), in_=words[z][:, a:b])
-
-        def load_f(eng):
-            eng.dma_start(out=f_right[:], in_=frac)
-
-        load_w(0, nc.sync)
-        load_s(0, nc.scalar)
-        load_w(1, nc.sync)
-        load_s(1, nc.scalar)
-        load_s(2, nc.sync)
-        load_s(3, nc.sync)
-        load_x(0, nc.sync)
-        load_x(1, nc.sync)
-        load_f(nc.sync)
+        for z in range(PASSES):
+            load_scales(z, nc.scalar)
+            nc.sync.dma_start(out=w_raw[z][:], in_=w_rows[z])
+        for r in range(SCALE_ROWS // 2, SCALE_ROWS):
+            load_scales(r, nc.sync)
+        for z in range(PASSES):
+            nc.sync.dma_start(
+                out=x_codes[z][:].bitcast(I32), in_=x_words[z].rearrange("p n t -> p (n t)").bitcast(I32)
+            )
+        nc.sync.dma_start(out=f_right[:], in_=frac)
         nc.sync.dma_start(right_offs[:], right)
         nc.sync.dma_start(left_offs[:], left)
 
-        w_codes = []
-        w_plane = []
-        grouped = []
+        w_bf16, w_codes, w_plane = [], [], []
         for z in range(PASSES):
-            grouped.append(keep.tile([P, N, PACK], BF16, name="grouped%d" % z, align_bytes=64))
+            w_bf16.append(keep.tile([P, N, PACK], BF16, name="w_bf16_%d" % z, align_bytes=64))
             w_codes.append(keep.tile([P, N], U32, name="w_codes%d" % z, align_bytes=64))
             w_plane.append(keep.tile([P, N], U8, name="w_plane%d" % z, align_bytes=64))
 
-        def cast(z, a, b, on_scalar):
-            dst = grouped[z][:, a:b, :].rearrange("p (c i) t -> p c t i", i=4)
-            src = w_raw[z][:].rearrange("p (t c i) -> p c t i", t=PACK, i=4)[:, a // 4 : b // 4, :, :]
-            if on_scalar:
-                nc.scalar.copy(out=dst, in_=src)
-            else:
-                nc.vector.tensor_copy(out=dst, in_=src)
-
-        def quant(z):
+        for z in range(PASSES):
+            nc.vector.tensor_copy(
+                out=w_bf16[z][:].rearrange("p (c i) t -> p c t i", i=RUN),
+                in_=w_raw[z][:].rearrange("p (t c i) -> p c t i", t=PACK, i=RUN),
+            )
             nc.vector.quantize_mx(
-                out=w_codes[z][:].bitcast(FP8X4), scales=w_plane[z][:], in_=grouped[z][:].rearrange("p m t -> p (m t)")
+                out=w_codes[z][:].bitcast(FP8X4), scales=w_plane[z][:], in_=w_bf16[z][:].rearrange("p m t -> p (m t)")
             )
 
-        cast(0, 0, N, False)
-        quant(0)
-        cast(1, 0, N, False)
-        quant(1)
-
-        banks = [psum.tile([P, b - a], F32, name="bank%d" % i) for i, (a, b) in enumerate(GROUPS)]
+        frame_cols = [slice(c, c + BANK_COLS) for c in range(0, T, BANK_COLS)]
+        banks = [psum.tile([P, BANK_COLS], F32, name="bank%d" % i) for i in range(len(frame_cols))]
         for z in range(PASSES):
-            for i, (a, b) in enumerate(GROUPS):
-                j = [n for n, (pz, pa, pb) in enumerate(XPIECES) if pz == z and pa <= a and b <= pb][0]
-                base = XPIECES[j][1]
+            for bank, cols in zip(banks, frame_cols):
                 nc.tensor.matmul_mx(
-                    out=banks[i][:],
+                    out=bank[:],
                     lhsT=w_codes[z][:].bitcast(FP8X4),
                     lhsT_scale=w_plane[z][:],
-                    rhs=x_tiles[j][:, a - base : b - base].bitcast(FP8X4),
-                    rhs_scale=x_plane[:, z, a:b],
+                    rhs=x_codes[z][:, cols].bitcast(FP8X4),
+                    rhs_scale=x_plane[:, z, cols],
                     start=(z == 0),
                     stop=(z == PASSES - 1),
                 )
 
-        y = keep.tile([P, T], F32, name="y")
-
-        def drain(i, on_scalar):
-            a, b = GROUPS[i]
-            if on_scalar:
-                nc.scalar.copy(out=y[:, a:b], in_=banks[i][:])
-            else:
-                nc.vector.tensor_copy(out=y[:, a:b], in_=banks[i][:])
-
-        for i in range(4):
-            drain(i, False)
+        y = keep.tile([P, T + SPARE], F32, name="y")
+        for bank, cols in zip(banks, frame_cols):
+            nc.vector.tensor_copy(out=y[:, cols], in_=bank[:])
 
         f_left = keep.tile([P, T], F32, name="f_left")
-        r = keep.tile([P, T], F32, name="r")
-        l = keep.tile([P, T], F32, name="l")
-        o = keep.tile([P, T], F32, name="o")
+        right_part = keep.tile([P, T], F32, name="right_part")
+        left_part = keep.tile([P, T], F32, name="left_part")
+        result = keep.tile([P, T], F32, name="result")
 
-        def comp(a, b):
-            nc.vector.tensor_scalar(f_left[:, a:b], f_right[:, a:b], -1.0, 1.0, MULT, ADD)
+        nc.vector.tensor_scalar(f_left[:], f_right[:], -1.0, 1.0, MULT, ADD)
 
-        def gr(a, b):
-            nc.vector.tensor_tensor(r[:, a:b], y[:].indirect(right_offs[:, a // 16 : b // 16]), f_right[:, a:b], MULT)
+        def gather_times(part, offs, factor, a, b):
+            nc.vector.tensor_tensor(part[:, a:b], y[:].indirect(offs[:, a // STRIPE : b // STRIPE]), factor[:, a:b], MULT)
 
-        def gl(a, b):
-            nc.vector.tensor_tensor(l[:, a:b], y[:].indirect(left_offs[:, a // 16 : b // 16]), f_left[:, a:b], MULT)
+        gather_times(right_part, right_offs, f_right, 0, T)
+        for a in (0, HALF):
+            gather_times(left_part, left_offs, f_left, a, a + HALF)
 
-        def add(a, b):
-            nc.vector.tensor_tensor(o[:, a:b], r[:, a:b], l[:, a:b], ADD)
-
-        def store(a, b, eng):
-            eng.dma_start(out=out[:, a:b], in_=o[:, a:b])
-
-        comp(0, 512)
-        gr(0, 256)
-        gl(0, 256)
-        gr(256, 512)
-        gl(256, 512)
-        add(0, 256)
-        store(0, 256, nc.scalar)
-        add(256, 512)
-        store(256, 512, nc.sync)
+        for a, queue in ((0, nc.scalar), (HALF, nc.sync)):
+            cols = slice(a, a + HALF)
+            nc.vector.tensor_tensor(result[:, cols], right_part[:, cols], left_part[:, cols], ADD)
+            queue.dma_start(out=out[:, cols], in_=result[:, cols])

@@ -35,7 +35,10 @@ def tile_picked_wlerp_none_l_kernel(tc, x_words, x_scales, w1, frac, left, right
 
         w_raw = [keep.tile([P, PACK * N], F32, name="w_raw%d" % z) for z in range(PASSES)]
         x_plane = keep.tile([P, PASSES, T], U8, name="x_plane", align_bytes=64)
-        x_codes = [keep.tile([P, T], U32, name="x_codes%d" % z, align_bytes=64) for z in range(PASSES)]
+        x_codes = [
+            [keep.tile([P, HALF], U32, name="x_codes%d_%d" % (z, h), align_bytes=64) for h in range(2)]
+            for z in range(PASSES)
+        ]
         f_right = keep.tile([P, T], F32, name="f_right")
         right_offs = keep.tile([P, T // STRIPE], U16, name="right_offs")
         left_offs = keep.tile([P, T // STRIPE], U16, name="left_offs")
@@ -48,15 +51,16 @@ def tile_picked_wlerp_none_l_kernel(tc, x_words, x_scales, w1, frac, left, right
                 in_=x_scales[:, r : P // 8 : SCALE_ROWS, :].rearrange("z q c -> q z c").bitcast(I32),
             )
 
+        for r in range(SCALE_ROWS):
+            load_scales(r, nc.sync if r == 1 else nc.scalar)
         for z in range(PASSES):
-            load_scales(z, nc.scalar)
             nc.sync.dma_start(out=w_raw[z][:], in_=w_rows[z])
-        for r in range(SCALE_ROWS // 2, SCALE_ROWS):
-            load_scales(r, nc.sync)
         for z in range(PASSES):
-            nc.sync.dma_start(
-                out=x_codes[z][:].bitcast(I32), in_=x_words[z].rearrange("p n t -> p (n t)").bitcast(I32)
-            )
+            for h in range(2):
+                nc.sync.dma_start(
+                    out=x_codes[z][h][:].bitcast(I32),
+                    in_=x_words[z].rearrange("p n t -> p (n t)").bitcast(I32)[:, h * HALF : (h + 1) * HALF],
+                )
         nc.sync.dma_start(out=f_right[:], in_=frac)
         nc.sync.dma_start(right_offs[:], right)
         nc.sync.dma_start(left_offs[:], left)
@@ -67,14 +71,19 @@ def tile_picked_wlerp_none_l_kernel(tc, x_words, x_scales, w1, frac, left, right
             w_codes.append(keep.tile([P, N], U32, name="w_codes%d" % z, align_bytes=64))
             w_plane.append(keep.tile([P, N], U8, name="w_plane%d" % z, align_bytes=64))
 
+        w_halves = [slice(0, N // 2), slice(N // 2, N)]
         for z in range(PASSES):
-            nc.vector.tensor_copy(
-                out=w_bf16[z][:].rearrange("p (c i) t -> p c t i", i=RUN),
-                in_=w_raw[z][:].rearrange("p (t c i) -> p c t i", t=PACK, i=RUN),
-            )
-            nc.vector.quantize_mx(
-                out=w_codes[z][:].bitcast(FP8X4), scales=w_plane[z][:], in_=w_bf16[z][:].rearrange("p m t -> p (m t)")
-            )
+            for cols in w_halves:
+                nc.vector.tensor_copy(
+                    out=w_bf16[z][:, cols, :].rearrange("p (c i) t -> p c t i", i=RUN),
+                    in_=w_raw[z][:].rearrange("p (t m) -> p t m", t=PACK)[:, :, cols].rearrange("p t (c i) -> p c t i", i=RUN),
+                )
+            for cols in w_halves:
+                nc.vector.quantize_mx(
+                    out=w_codes[z][:, cols].bitcast(FP8X4),
+                    scales=w_plane[z][:, cols],
+                    in_=w_bf16[z][:, cols, :].rearrange("p m t -> p (m t)"),
+                )
 
         frame_cols = [slice(c, c + BANK_COLS) for c in range(0, T, BANK_COLS)]
         banks = [psum.tile([P, BANK_COLS], F32, name="bank%d" % i) for i in range(len(frame_cols))]
@@ -84,7 +93,7 @@ def tile_picked_wlerp_none_l_kernel(tc, x_words, x_scales, w1, frac, left, right
                     out=bank[:],
                     lhsT=w_codes[z][:].bitcast(FP8X4),
                     lhsT_scale=w_plane[z][:],
-                    rhs=x_codes[z][:, cols].bitcast(FP8X4),
+                    rhs=x_codes[z][cols.start // HALF][:, cols.start % HALF : cols.start % HALF + BANK_COLS].bitcast(FP8X4),
                     rhs_scale=x_plane[:, z, cols],
                     start=(z == 0),
                     stop=(z == PASSES - 1),

@@ -51,10 +51,11 @@ def tile_picked_wlerp_none_l_kernel(tc, x_words, x_scales, w1, frac, left, right
                 in_=x_scales[:, r : P // 8 : SCALE_ROWS, :].rearrange("z q c -> q z c").bitcast(I32),
             )
 
-        for r in range(SCALE_ROWS):
-            load_scales(r, nc.sync if r == 1 else nc.scalar)
-        for z in range(PASSES):
-            nc.sync.dma_start(out=w_raw[z][:], in_=w_rows[z])
+        for r in range(SCALE_ROWS - 1):
+            load_scales(r, nc.scalar)
+        nc.sync.dma_start(out=w_raw[0][:], in_=w_rows[0])
+        load_scales(SCALE_ROWS - 1, nc.sync)
+        nc.sync.dma_start(out=w_raw[1][:], in_=w_rows[1])
         for z in range(PASSES):
             for h in range(2):
                 nc.sync.dma_start(

@@ -118,7 +118,7 @@ def tile_picked_wlerp_none_l_kernel(tc, x_words, x_scales, w1, frac, left, right
         for a in (0, HALF):
             gather_times(left_part, left_offs, f_left, a, a + HALF)
 
-        for a, queue in ((0, nc.scalar), (HALF, nc.sync)):
+        for a in (0, HALF):
             cols = slice(a, a + HALF)
             nc.vector.tensor_tensor(result[:, cols], right_part[:, cols], left_part[:, cols], ADD)
-            queue.dma_start(out=out[:, cols], in_=result[:, cols])
+            nc.sync.dma_start(out=out[:, cols], in_=result[:, cols])

@@ -35,9 +35,9 @@ def tile_picked_wlerp_none_l_kernel(tc, x_words, x_scales, w1, frac, left, right
 
         w_raw = [keep.tile([P, PACK * N], F32, name="w_raw%d" % z) for z in range(PASSES)]
         x_plane = keep.tile([P, PASSES, T], U8, name="x_plane", align_bytes=64)
+        x_pieces = [(0, 0, HALF), (0, HALF, T), (1, 0, HALF), (1, HALF, T - BANK_COLS), (1, T - BANK_COLS, T)]
         x_codes = [
-            [keep.tile([P, HALF], U32, name="x_codes%d_%d" % (z, h), align_bytes=64) for h in range(2)]
-            for z in range(PASSES)
+            keep.tile([P, b - a], U32, name="x_codes%d_%d" % (z, a), align_bytes=64) for z, a, b in x_pieces
         ]
         f_right = keep.tile([P, T], F32, name="f_right")
         right_offs = keep.tile([P, T // STRIPE], U16, name="right_offs")
@@ -56,12 +56,10 @@ def tile_picked_wlerp_none_l_kernel(tc, x_words, x_scales, w1, frac, left, right
         nc.sync.dma_start(out=w_raw[0][:], in_=w_rows[0])
         load_scales(SCALE_ROWS - 1, nc.sync)
         nc.sync.dma_start(out=w_raw[1][:], in_=w_rows[1])
-        for z in range(PASSES):
-            for h in range(2):
-                nc.sync.dma_start(
-                    out=x_codes[z][h][:].bitcast(I32),
-                    in_=x_words[z].rearrange("p n t -> p (n t)").bitcast(I32)[:, h * HALF : (h + 1) * HALF],
-                )
+        for codes, (z, a, b) in zip(x_codes, x_pieces):
+            nc.sync.dma_start(
+                out=codes[:].bitcast(I32), in_=x_words[z].rearrange("p n t -> p (n t)").bitcast(I32)[:, a:b]
+            )
         nc.sync.dma_start(out=f_right[:], in_=frac)
         nc.sync.dma_start(right_offs[:], right)
         nc.sync.dma_start(left_offs[:], left)
@@ -88,13 +86,14 @@ def tile_picked_wlerp_none_l_kernel(tc, x_words, x_scales, w1, frac, left, right
 
         frame_cols = [slice(c, c + BANK_COLS) for c in range(0, T, BANK_COLS)]
         banks = [psum.tile([P, BANK_COLS], F32, name="bank%d" % i) for i in range(len(frame_cols))]
-        for z in range(PASSES):
-            for bank, cols in zip(banks, frame_cols):
+        for codes, (z, a, b) in zip(x_codes, x_pieces):
+            for c in range(a, b, BANK_COLS):
+                bank, cols = banks[c // BANK_COLS], frame_cols[c // BANK_COLS]
                 nc.tensor.matmul_mx(
                     out=bank[:],
                     lhsT=w_codes[z][:].bitcast(FP8X4),
                     lhsT_scale=w_plane[z][:],
-                    rhs=x_codes[z][cols.start // HALF][:, cols.start % HALF : cols.start % HALF + BANK_COLS].bitcast(FP8X4),
+                    rhs=codes[:, c - a : c - a + BANK_COLS].bitcast(FP8X4),
                     rhs_scale=x_plane[:, z, cols],
                     start=(z == 0),
                     stop=(z == PASSES - 1),

@@ -51,10 +51,10 @@ def tile_picked_wlerp_none_l_kernel(tc, x_words, x_scales, w1, frac, left, right
                 in_=x_scales[:, r : P // 8 : SCALE_ROWS, :].rearrange("z q c -> q z c").bitcast(I32),
             )
 
-        for r in range(SCALE_ROWS - 1):
-            load_scales(r, nc.scalar)
+        load_scales(0, nc.scalar)
         nc.sync.dma_start(out=w_raw[0][:], in_=w_rows[0])
-        load_scales(SCALE_ROWS - 1, nc.sync)
+        for r in range(1, SCALE_ROWS):
+            load_scales(r, nc.sync)
         nc.sync.dma_start(out=w_raw[1][:], in_=w_rows[1])
         for codes, (z, a, b) in zip(x_codes, x_pieces):
             nc.sync.dma_start(

@@ -13,7 +13,8 @@ U16 = mybir.dt.uint16
 U8 = mybir.dt.uint8
 FP8X4 = mybir.dt.float8_e4m3fn_x4
 MULT = mybir.AluOpType.mult
-ADD = mybir.AluOpType.add
+SUB = mybir.AluOpType.subtract
+COPY = mybir.ActivationFunctionType.Copy
 
 P = 128
 PACK = 4
@@ -100,24 +101,22 @@ def tile_picked_wlerp_none_l_kernel(tc, x_words, x_scales, w1, frac, left, right
                 )
 
         y = keep.tile([P, T + SPARE], F32, name="y")
-        for bank, cols in zip(banks, frame_cols):
+        nc.scalar.activation(y[:, frame_cols[0]], banks[0][:], COPY)
+        for bank, cols in zip(banks[1:], frame_cols[1:]):
             nc.vector.tensor_copy(out=y[:, cols], in_=bank[:])
 
-        f_left = keep.tile([P, T], F32, name="f_left")
         right_part = keep.tile([P, T], F32, name="right_part")
+        left_cols = keep.tile([P, T], F32, name="left_cols")
         left_part = keep.tile([P, T], F32, name="left_part")
         result = keep.tile([P, T], F32, name="result")
 
-        nc.vector.tensor_scalar(f_left[:], f_right[:], -1.0, 1.0, MULT, ADD)
-
-        def gather_times(part, offs, factor, a, b):
-            nc.vector.tensor_tensor(part[:, a:b], y[:].indirect(offs[:, a // STRIPE : b // STRIPE]), factor[:, a:b], MULT)
-
-        gather_times(right_part, right_offs, f_right, 0, T)
-        for a in (0, HALF):
-            gather_times(left_part, left_offs, f_left, a, a + HALF)
-
-        for a in (0, HALF):
-            cols = slice(a, a + HALF)
-            nc.vector.tensor_tensor(result[:, cols], right_part[:, cols], left_part[:, cols], ADD)
+        nc.vector.tensor_tensor(right_part[:], y[:].indirect(right_offs[:]), f_right[:], MULT)
+        halves = [slice(a, a + HALF) for a in (0, HALF)]
+        for cols in halves:
+            offs = left_offs[:, cols.start // STRIPE : cols.stop // STRIPE]
+            nc.scalar.activation(left_cols[:, cols], y[:].indirect(offs), COPY)
+        for cols in halves:
+            nc.vector.scalar_tensor_tensor(left_part[:, cols], f_right[:, cols], 1.0, left_cols[:, cols], SUB, MULT)
+        for cols in halves:
+            nc.vector.tensor_tensor(result[:, cols], right_part[:, cols], left_part[:, cols], SUB)
             nc.sync.dma_start(out=out[:, cols], in_=result[:, cols])

@@ -25,6 +25,8 @@ STRIPE = 16
 RUN = 4
 BANK_COLS = 128
 HALF = T // 2
+LAST = 64
+SCALAR_COLS = 32
 SPARE = 16
 
 
@@ -72,12 +74,19 @@ def tile_picked_wlerp_none_l_kernel(tc, x_words, x_scales, w1, frac, left, right
             w_plane.append(keep.tile([P, N], U8, name="w_plane%d" % z, align_bytes=64))
 
         w_halves = [slice(0, N // 2), slice(N // 2, N)]
+
+        def interleave_views(z, cols):
+            return (
+                w_bf16[z][:, cols, :].rearrange("p (c i) t -> p c t i", i=RUN),
+                w_raw[z][:].rearrange("p (t m) -> p t m", t=PACK)[:, :, cols].rearrange("p t (c i) -> p c t i", i=RUN),
+            )
+
         for z in range(PASSES):
-            for cols in w_halves:
-                nc.vector.tensor_copy(
-                    out=w_bf16[z][:, cols, :].rearrange("p (c i) t -> p c t i", i=RUN),
-                    in_=w_raw[z][:].rearrange("p (t m) -> p t m", t=PACK)[:, :, cols].rearrange("p t (c i) -> p c t i", i=RUN),
-                )
+            shared = SCALAR_COLS if z == PASSES - 1 else 0
+            nc.vector.tensor_copy(*interleave_views(z, w_halves[0]))
+            nc.vector.tensor_copy(*interleave_views(z, slice(N // 2, N - shared)))
+            if shared:
+                nc.scalar.activation(*interleave_views(z, slice(N - shared, N)), COPY)
             for cols in w_halves:
                 nc.vector.quantize_mx(
                     out=w_codes[z][:, cols].bitcast(FP8X4),
@@ -101,8 +110,7 @@ def tile_picked_wlerp_none_l_kernel(tc, x_words, x_scales, w1, frac, left, right
                 )
 
         y = keep.tile([P, T + SPARE], F32, name="y")
-        nc.scalar.activation(y[:, frame_cols[0]], banks[0][:], COPY)
-        for bank, cols in zip(banks[1:], frame_cols[1:]):
+        for bank, cols in zip(banks, frame_cols):
             nc.vector.tensor_copy(out=y[:, cols], in_=bank[:])
 
         right_part = keep.tile([P, T], F32, name="right_part")
@@ -111,12 +119,21 @@ def tile_picked_wlerp_none_l_kernel(tc, x_words, x_scales, w1, frac, left, right
         result = keep.tile([P, T], F32, name="result")
 
         nc.vector.tensor_tensor(right_part[:], y[:].indirect(right_offs[:]), f_right[:], MULT)
-        halves = [slice(a, a + HALF) for a in (0, HALF)]
-        for cols in halves:
+        first, third, last = slice(0, HALF), slice(HALF, T - LAST), slice(T - LAST, T)
+        for cols in (first, third, last):
             offs = left_offs[:, cols.start // STRIPE : cols.stop // STRIPE]
             nc.scalar.activation(left_cols[:, cols], y[:].indirect(offs), COPY)
-        for cols in halves:
+
+        def weigh_left(cols):
             nc.vector.scalar_tensor_tensor(left_part[:, cols], f_right[:, cols], 1.0, left_cols[:, cols], SUB, MULT)
-        for cols in halves:
+
+        def combine(cols):
             nc.vector.tensor_tensor(result[:, cols], right_part[:, cols], left_part[:, cols], SUB)
-            nc.sync.dma_start(out=out[:, cols], in_=result[:, cols])
+
+        weigh_left(first)
+        weigh_left(third)
+        combine(first)
+        nc.sync.dma_start(out=out[:, first], in_=result[:, first])
+        weigh_left(last)
+        combine(slice(HALF, T))
+        nc.sync.dma_start(out=out[:, HALF:T], in_=result[:, HALF:T])

@@ -54,9 +54,10 @@ def tile_picked_wlerp_none_l_kernel(tc, x_words, x_scales, w1, frac, left, right
                 in_=x_scales[:, r : P // 8 : SCALE_ROWS, :].rearrange("z q c -> q z c").bitcast(I32),
             )
 
-        load_scales(0, nc.scalar)
+        for r in range(SCALE_ROWS // 2):
+            load_scales(r, nc.scalar)
         nc.sync.dma_start(out=w_raw[0][:], in_=w_rows[0])
-        for r in range(1, SCALE_ROWS):
+        for r in range(SCALE_ROWS // 2, SCALE_ROWS):
             load_scales(r, nc.sync)
         nc.sync.dma_start(out=w_raw[1][:], in_=w_rows[1])
         for codes, (z, a, b) in zip(x_codes, x_pieces):

@@ -27,6 +27,7 @@ BANK_COLS = 128
 HALF = T // 2
 LAST = 64
 SCALAR_COLS = 32
+ALIGN = 256
 SPARE = 16
 
 
@@ -36,13 +37,13 @@ def tile_picked_wlerp_none_l_kernel(tc, x_words, x_scales, w1, frac, left, right
         keep = ctx.enter_context(tc.tile_pool(name="keep", bufs=1))
         psum = ctx.enter_context(tc.psum_pool(name="psum", bufs=1))
 
-        w_raw = [keep.tile([P, PACK * N], F32, name="w_raw%d" % z) for z in range(PASSES)]
-        x_plane = keep.tile([P, PASSES, T], U8, name="x_plane", align_bytes=64)
+        w_raw = [keep.tile([P, PACK * N], F32, name="w_raw%d" % z, align_bytes=ALIGN) for z in range(PASSES)]
+        x_plane = keep.tile([P, PASSES, T], U8, name="x_plane", align_bytes=ALIGN)
         x_pieces = [(0, 0, HALF), (0, HALF, T), (1, 0, HALF), (1, HALF, T - BANK_COLS), (1, T - BANK_COLS, T)]
         x_codes = [
-            keep.tile([P, b - a], U32, name="x_codes%d_%d" % (z, a), align_bytes=64) for z, a, b in x_pieces
+            keep.tile([P, b - a], U32, name="x_codes%d_%d" % (z, a), align_bytes=ALIGN) for z, a, b in x_pieces
         ]
-        f_right = keep.tile([P, T], F32, name="f_right")
+        f_right = keep.tile([P, T], F32, name="f_right", align_bytes=ALIGN)
         right_offs = keep.tile([P, T // STRIPE], U16, name="right_offs")
         left_offs = keep.tile([P, T // STRIPE], U16, name="left_offs")
 
@@ -70,9 +71,9 @@ def tile_picked_wlerp_none_l_kernel(tc, x_words, x_scales, w1, frac, left, right
 
         w_bf16, w_codes, w_plane = [], [], []
         for z in range(PASSES):
-            w_bf16.append(keep.tile([P, N, PACK], BF16, name="w_bf16_%d" % z, align_bytes=64))
-            w_codes.append(keep.tile([P, N], U32, name="w_codes%d" % z, align_bytes=64))
-            w_plane.append(keep.tile([P, N], U8, name="w_plane%d" % z, align_bytes=64))
+            w_bf16.append(keep.tile([P, N, PACK], BF16, name="w_bf16_%d" % z, align_bytes=ALIGN))
+            w_codes.append(keep.tile([P, N], U32, name="w_codes%d" % z, align_bytes=ALIGN))
+            w_plane.append(keep.tile([P, N], U8, name="w_plane%d" % z, align_bytes=ALIGN))
 
         w_halves = [slice(0, N // 2), slice(N // 2, N)]
 
@@ -110,14 +111,14 @@ def tile_picked_wlerp_none_l_kernel(tc, x_words, x_scales, w1, frac, left, right
                     stop=(z == PASSES - 1),
                 )
 
-        y = keep.tile([P, T + SPARE], F32, name="y")
+        y = keep.tile([P, T + SPARE], F32, name="y", align_bytes=ALIGN)
         for bank, cols in zip(banks, frame_cols):
             nc.vector.tensor_copy(out=y[:, cols], in_=bank[:])
 
-        right_part = keep.tile([P, T], F32, name="right_part")
-        left_cols = keep.tile([P, T], F32, name="left_cols")
-        left_part = keep.tile([P, T], F32, name="left_part")
-        result = keep.tile([P, T], F32, name="result")
+        right_part = keep.tile([P, T], F32, name="right_part", align_bytes=ALIGN)
+        left_cols = keep.tile([P, T], F32, name="left_cols", align_bytes=ALIGN)
+        left_part = keep.tile([P, T], F32, name="left_part", align_bytes=ALIGN)
+        result = keep.tile([P, T], F32, name="result", align_bytes=ALIGN)
 
         nc.vector.tensor_tensor(right_part[:], y[:].indirect(right_offs[:]), f_right[:], MULT)
         first, third, last = slice(0, HALF), slice(HALF, T - LAST), slice(T - LAST, T)

@@ -27,7 +27,7 @@ BANK_COLS = 128
 HALF = T // 2
 LAST = 64
 SCALAR_COLS = 32
-ALIGN = 256
+ALIGN = 2048
 SPARE = 16
 
 

@@ -55,10 +55,9 @@ def tile_picked_wlerp_none_l_kernel(tc, x_words, x_scales, w1, frac, left, right
                 in_=x_scales[:, r : P // 8 : SCALE_ROWS, :].rearrange("z q c -> q z c").bitcast(I32),
             )
 
-        for r in range(SCALE_ROWS // 2):
-            load_scales(r, nc.scalar)
+        load_scales(0, nc.scalar)
         nc.sync.dma_start(out=w_raw[0][:], in_=w_rows[0])
-        for r in range(SCALE_ROWS // 2, SCALE_ROWS):
+        for r in range(1, SCALE_ROWS):
             load_scales(r, nc.sync)
         nc.sync.dma_start(out=w_raw[1][:], in_=w_rows[1])
         for codes, (z, a, b) in zip(x_codes, x_pieces):

@@ -64,9 +64,9 @@ def tile_picked_wlerp_none_l_kernel(tc, x_words, x_scales, w1, frac, left, right
             nc.sync.dma_start(
                 out=codes[:].bitcast(I32), in_=x_words[z].rearrange("p n t -> p (n t)").bitcast(I32)[:, a:b]
             )
-        nc.sync.dma_start(out=f_right[:], in_=frac)
-        nc.sync.dma_start(right_offs[:], right)
         nc.sync.dma_start(left_offs[:], left)
+        nc.sync.dma_start(right_offs[:], right)
+        nc.sync.dma_start(out=f_right[:], in_=frac)
 
         w_bf16, w_codes, w_plane = [], [], []
         for z in range(PASSES):

@@ -39,7 +39,7 @@ def tile_picked_wlerp_none_l_kernel(tc, x_words, x_scales, w1, frac, left, right
 
         w_raw = [keep.tile([P, PACK * N], F32, name="w_raw%d" % z, align_bytes=ALIGN) for z in range(PASSES)]
         x_plane = keep.tile([P, PASSES, T], U8, name="x_plane", align_bytes=ALIGN)
-        x_pieces = [(0, 0, HALF), (0, HALF, T), (1, 0, HALF), (1, HALF, T - BANK_COLS), (1, T - BANK_COLS, T)]
+        x_pieces = [(0, 0, HALF), (0, HALF, T), (1, 0, BANK_COLS), (1, BANK_COLS, T - BANK_COLS), (1, T - BANK_COLS, T)]
         x_codes = [
             keep.tile([P, b - a], U32, name="x_codes%d_%d" % (z, a), align_bytes=ALIGN) for z, a, b in x_pieces
         ]
@@ -57,9 +57,10 @@ def tile_picked_wlerp_none_l_kernel(tc, x_words, x_scales, w1, frac, left, right
 
         load_scales(0, nc.scalar)
         nc.sync.dma_start(out=w_raw[0][:], in_=w_rows[0])
-        for r in range(1, SCALE_ROWS):
-            load_scales(r, nc.sync)
+        load_scales(1, nc.sync)
         nc.sync.dma_start(out=w_raw[1][:], in_=w_rows[1])
+        for r in range(2, SCALE_ROWS):
+            load_scales(r, nc.sync)
         for codes, (z, a, b) in zip(x_codes, x_pieces):
             nc.sync.dma_start(
                 out=codes[:].bitcast(I32), in_=x_words[z].rearrange("p n t -> p (n t)").bitcast(I32)[:, a:b]
@@ -82,18 +83,22 @@ def tile_picked_wlerp_none_l_kernel(tc, x_words, x_scales, w1, frac, left, right
                 w_raw[z][:].rearrange("p (t m) -> p t m", t=PACK)[:, :, cols].rearrange("p t (c i) -> p c t i", i=RUN),
             )
 
-        for z in range(PASSES):
-            shared = SCALAR_COLS if z == PASSES - 1 else 0
-            nc.vector.tensor_copy(*interleave_views(z, w_halves[0]))
-            nc.vector.tensor_copy(*interleave_views(z, slice(N // 2, N - shared)))
-            if shared:
-                nc.scalar.activation(*interleave_views(z, slice(N - shared, N)), COPY)
-            for cols in w_halves:
-                nc.vector.quantize_mx(
-                    out=w_codes[z][:, cols].bitcast(FP8X4),
-                    scales=w_plane[z][:, cols],
-                    in_=w_bf16[z][:, cols, :].rearrange("p m t -> p (m t)"),
-                )
+        def quantize(z, cols):
+            nc.vector.quantize_mx(
+                out=w_codes[z][:, cols].bitcast(FP8X4),
+                scales=w_plane[z][:, cols],
+                in_=w_bf16[z][:, cols, :].rearrange("p m t -> p (m t)"),
+            )
+
+        for cols in w_halves:
+            nc.vector.tensor_copy(*interleave_views(0, cols))
+        for cols in w_halves:
+            quantize(0, cols)
+        nc.scalar.activation(*interleave_views(1, slice(N - SCALAR_COLS, N)), COPY)
+        nc.vector.tensor_copy(*interleave_views(1, slice(N // 2, N - SCALAR_COLS)))
+        nc.vector.tensor_copy(*interleave_views(1, w_halves[0]))
+        quantize(1, w_halves[1])
+        quantize(1, w_halves[0])
 
         frame_cols = [slice(c, c + BANK_COLS) for c in range(0, T, BANK_COLS)]
         banks = [psum.tile([P, BANK_COLS], F32, name="bank%d" % i) for i in range(len(frame_cols))]

@@ -23,9 +23,7 @@ QUADRANT = 32
 SCALE_ROWS = 4
 STRIPE = 16
 RUN = 4
-BANK_COLS = 128
-HALF = T // 2
-LAST = 64
+BANK = 128
 SCALAR_COLS = 32
 ALIGN = 2048
 SPARE = 16
@@ -39,15 +37,17 @@ def tile_picked_wlerp_none_l_kernel(tc, x_words, x_scales, w1, frac, left, right
 
         w_raw = [keep.tile([P, PACK * N], F32, name="w_raw%d" % z, align_bytes=ALIGN) for z in range(PASSES)]
         x_plane = keep.tile([P, PASSES, T], U8, name="x_plane", align_bytes=ALIGN)
-        x_pieces = [(0, 0, HALF), (0, HALF, T), (1, 0, BANK_COLS), (1, BANK_COLS, T - BANK_COLS), (1, T - BANK_COLS, T)]
+        x_pieces = [(0, 1, 0, 3 * BANK), (0, 2, 3 * BANK, T), (1, 2, 0, 2 * BANK), (1, 2, 2 * BANK, 3 * BANK)]
         x_codes = [
-            keep.tile([P, b - a], U32, name="x_codes%d_%d" % (z, a), align_bytes=ALIGN) for z, a, b in x_pieces
+            keep.tile([P, z1 - z0, b - a], U32, name="x_codes%d" % i, align_bytes=ALIGN)
+            for i, (z0, z1, a, b) in enumerate(x_pieces)
         ]
         f_right = keep.tile([P, T], F32, name="f_right", align_bytes=ALIGN)
         right_offs = keep.tile([P, T // STRIPE], U16, name="right_offs")
         left_offs = keep.tile([P, T // STRIPE], U16, name="left_offs")
 
         w_rows = w1.rearrange("(z p t) m -> z p (t m)", z=PASSES, t=PACK)
+        x_rows = x_words.rearrange("z p n t -> p z (n t)").bitcast(I32)
 
         def load_scales(r, queue):
             queue.dma_start(
@@ -55,16 +55,18 @@ def tile_picked_wlerp_none_l_kernel(tc, x_words, x_scales, w1, frac, left, right
                 in_=x_scales[:, r : P // 8 : SCALE_ROWS, :].rearrange("z q c -> q z c").bitcast(I32),
             )
 
+        def load_x(i):
+            z0, z1, a, b = x_pieces[i]
+            nc.sync.dma_start(out=x_codes[i][:].bitcast(I32), in_=x_rows[:, z0:z1, a:b])
+
         load_scales(0, nc.scalar)
         nc.sync.dma_start(out=w_raw[0][:], in_=w_rows[0])
         load_scales(1, nc.sync)
         nc.sync.dma_start(out=w_raw[1][:], in_=w_rows[1])
         for r in range(2, SCALE_ROWS):
             load_scales(r, nc.sync)
-        for codes, (z, a, b) in zip(x_codes, x_pieces):
-            nc.sync.dma_start(
-                out=codes[:].bitcast(I32), in_=x_words[z].rearrange("p n t -> p (n t)").bitcast(I32)[:, a:b]
-            )
+        for i in range(len(x_pieces)):
+            load_x(i)
         nc.sync.dma_start(left_offs[:], left)
         nc.sync.dma_start(right_offs[:], right)
         nc.sync.dma_start(out=f_right[:], in_=frac)
@@ -100,46 +102,54 @@ def tile_picked_wlerp_none_l_kernel(tc, x_words, x_scales, w1, frac, left, right
         quantize(1, w_halves[1])
         quantize(1, w_halves[0])
 
-        frame_cols = [slice(c, c + BANK_COLS) for c in range(0, T, BANK_COLS)]
-        banks = [psum.tile([P, BANK_COLS], F32, name="bank%d" % i) for i in range(len(frame_cols))]
-        for codes, (z, a, b) in zip(x_codes, x_pieces):
-            for c in range(a, b, BANK_COLS):
-                bank, cols = banks[c // BANK_COLS], frame_cols[c // BANK_COLS]
-                nc.tensor.matmul_mx(
-                    out=bank[:],
-                    lhsT=w_codes[z][:].bitcast(FP8X4),
-                    lhsT_scale=w_plane[z][:],
-                    rhs=codes[:, c - a : c - a + BANK_COLS].bitcast(FP8X4),
-                    rhs_scale=x_plane[:, z, cols],
-                    start=(z == 0),
-                    stop=(z == PASSES - 1),
-                )
-
+        banks = [psum.tile([P, BANK], F32, name="bank%d" % i) for i in range(T // BANK)]
         y = keep.tile([P, T + SPARE], F32, name="y", align_bytes=ALIGN)
-        for bank, cols in zip(banks, frame_cols):
-            nc.vector.tensor_copy(out=y[:, cols], in_=bank[:])
+        for codes, (z0, z1, a, b) in zip(x_codes, x_pieces):
+            for z in range(z0, z1):
+                for c in range(a, b, BANK):
+                    nc.tensor.matmul_mx(
+                        out=banks[c // BANK][:],
+                        lhsT=w_codes[z][:].bitcast(FP8X4),
+                        lhsT_scale=w_plane[z][:],
+                        rhs=codes[:, z - z0, c - a : c - a + BANK].bitcast(FP8X4),
+                        rhs_scale=x_plane[:, z, c : c + BANK],
+                        start=(z == 0),
+                        stop=(z == PASSES - 1),
+                    )
+                    if z == PASSES - 1:
+                        nc.vector.tensor_copy(out=y[:, c : c + BANK], in_=banks[c // BANK][:])
 
         right_part = keep.tile([P, T], F32, name="right_part", align_bytes=ALIGN)
         left_cols = keep.tile([P, T], F32, name="left_cols", align_bytes=ALIGN)
         left_part = keep.tile([P, T], F32, name="left_part", align_bytes=ALIGN)
         result = keep.tile([P, T], F32, name="result", align_bytes=ALIGN)
 
-        nc.vector.tensor_tensor(right_part[:], y[:].indirect(right_offs[:]), f_right[:], MULT)
-        first, third, last = slice(0, HALF), slice(HALF, T - LAST), slice(T - LAST, T)
-        for cols in (first, third, last):
-            offs = left_offs[:, cols.start // STRIPE : cols.stop // STRIPE]
-            nc.scalar.activation(left_cols[:, cols], y[:].indirect(offs), COPY)
+        def gather_right(a, b):
+            offs = right_offs[:, a // STRIPE : b // STRIPE]
+            nc.vector.tensor_tensor(right_part[:, a:b], y[:].indirect(offs), f_right[:, a:b], MULT)
 
-        def weigh_left(cols):
-            nc.vector.scalar_tensor_tensor(left_part[:, cols], f_right[:, cols], 1.0, left_cols[:, cols], SUB, MULT)
+        def gather_left(a, b):
+            nc.scalar.activation(left_cols[:, a:b], y[:].indirect(left_offs[:, a // STRIPE : b // STRIPE]), COPY)
 
-        def combine(cols):
-            nc.vector.tensor_tensor(result[:, cols], right_part[:, cols], left_part[:, cols], SUB)
+        def weigh_left(a, b):
+            nc.vector.scalar_tensor_tensor(left_part[:, a:b], f_right[:, a:b], 1.0, left_cols[:, a:b], SUB, MULT)
 
-        weigh_left(first)
-        weigh_left(third)
-        combine(first)
-        nc.sync.dma_start(out=out[:, first], in_=result[:, first])
-        weigh_left(last)
-        combine(slice(HALF, T))
-        nc.sync.dma_start(out=out[:, HALF:T], in_=result[:, HALF:T])
+        def combine(a, b):
+            nc.vector.tensor_tensor(result[:, a:b], right_part[:, a:b], left_part[:, a:b], SUB)
+
+        def store(a, b):
+            nc.sync.dma_start(out=out[:, a:b], in_=result[:, a:b])
+
+        gather_right(0, T)
+        weighed = [(0, 128), (128, 384), (384, T)]
+        stored = [(0, 128), (128, 320), (320, T)]
+        for cut in weighed:
+            gather_left(*cut)
+        weigh_left(*weighed[0])
+        weigh_left(*weighed[1])
+        combine(*stored[0])
+        store(*stored[0])
+        weigh_left(*weighed[2])
+        for cut in stored[1:]:
+            combine(*cut)
+            store(*cut)

@@ -37,7 +37,7 @@ def tile_picked_wlerp_none_l_kernel(tc, x_words, x_scales, w1, frac, left, right
 
         w_raw = [keep.tile([P, PACK * N], F32, name="w_raw%d" % z, align_bytes=ALIGN) for z in range(PASSES)]
         x_plane = keep.tile([P, PASSES, T], U8, name="x_plane", align_bytes=ALIGN)
-        x_pieces = [(0, 1, 0, 3 * BANK), (0, 2, 3 * BANK, T), (1, 2, 0, 2 * BANK), (1, 2, 2 * BANK, 3 * BANK)]
+        x_pieces = [(z, z + 1, a, a + T // 2) for z in range(PASSES) for a in (0, T // 2)]
         x_codes = [
             keep.tile([P, z1 - z0, b - a], U32, name="x_codes%d" % i, align_bytes=ALIGN)
             for i, (z0, z1, a, b) in enumerate(x_pieces)

@@ -117,7 +117,7 @@ def tile_picked_wlerp_none_l_kernel(tc, x_words, x_scales, w1, frac, left, right
                         stop=(z == PASSES - 1),
                     )
                     if z == PASSES - 1:
-                        nc.vector.tensor_copy(out=y[:, c : c + BANK], in_=banks[c // BANK][:])
+                        nc.scalar.copy(out=y[:, c : c + BANK], in_=banks[c // BANK][:])
 
         right_part = keep.tile([P, T], F32, name="right_part", align_bytes=ALIGN)
         left_cols = keep.tile([P, T], F32, name="left_cols", align_bytes=ALIGN)

from contextlib import ExitStack

import concourse.mybir as mybir

K, T, N = 1024, 512, 128
FLOPS = 2 * K * T * N

F32 = mybir.dt.float32
BF16 = mybir.dt.bfloat16
I32 = mybir.dt.int32
U32 = mybir.dt.uint32
U16 = mybir.dt.uint16
U8 = mybir.dt.uint8
FP8X4 = mybir.dt.float8_e4m3fn_x4
MULT = mybir.AluOpType.mult
SUB = mybir.AluOpType.subtract
COPY = mybir.ActivationFunctionType.Copy

P = 128
PACK = 4
PASSES = K // (P * PACK)
QUADRANT = 32
SCALE_ROWS = 4
STRIPE = 16
RUN = 4
BANK = 128
SCALAR_COLS = 32
ALIGN = 2048
SPARE = 16


def tile_picked_wlerp_none_l_kernel(tc, x_words, x_scales, w1, frac, left, right, out):
    nc = tc.nc
    with ExitStack() as ctx:
        keep = ctx.enter_context(tc.tile_pool(name="keep", bufs=1))
        psum = ctx.enter_context(tc.psum_pool(name="psum", bufs=1))

        w_raw = [keep.tile([P, PACK * N], F32, name="w_raw%d" % z, align_bytes=ALIGN) for z in range(PASSES)]
        x_plane = keep.tile([P, PASSES, T], U8, name="x_plane", align_bytes=ALIGN)
        x_pieces = [(z, z + 1, a, a + T // 2) for z in range(PASSES) for a in (0, T // 2)]
        x_codes = [
            keep.tile([P, z1 - z0, b - a], U32, name="x_codes%d" % i, align_bytes=ALIGN)
            for i, (z0, z1, a, b) in enumerate(x_pieces)
        ]
        f_right = keep.tile([P, T], F32, name="f_right", align_bytes=ALIGN)
        right_offs = keep.tile([P, T // STRIPE], U16, name="right_offs")
        left_offs = keep.tile([P, T // STRIPE], U16, name="left_offs")

        w_rows = w1.rearrange("(z p t) m -> z p (t m)", z=PASSES, t=PACK)
        x_rows = x_words.rearrange("z p n t -> p z (n t)").bitcast(I32)

        def load_scales(r, queue):
            queue.dma_start(
                out=x_plane[r:P:QUADRANT, :, :].bitcast(I32),
                in_=x_scales[:, r : P // 8 : SCALE_ROWS, :].rearrange("z q c -> q z c").bitcast(I32),
            )

        def load_x(i):
            z0, z1, a, b = x_pieces[i]
            nc.sync.dma_start(out=x_codes[i][:].bitcast(I32), in_=x_rows[:, z0:z1, a:b])

        load_scales(0, nc.scalar)
        nc.sync.dma_start(out=w_raw[0][:], in_=w_rows[0])
        load_scales(1, nc.sync)
        nc.sync.dma_start(out=w_raw[1][:], in_=w_rows[1])
        for r in range(2, SCALE_ROWS):
            load_scales(r, nc.sync)
        for i in range(len(x_pieces)):
            load_x(i)
        nc.sync.dma_start(left_offs[:], left)
        nc.sync.dma_start(right_offs[:], right)
        nc.sync.dma_start(out=f_right[:], in_=frac)

        w_bf16, w_codes, w_plane = [], [], []
        for z in range(PASSES):
            w_bf16.append(keep.tile([P, N, PACK], BF16, name="w_bf16_%d" % z, align_bytes=ALIGN))
            w_codes.append(keep.tile([P, N], U32, name="w_codes%d" % z, align_bytes=ALIGN))
            w_plane.append(keep.tile([P, N], U8, name="w_plane%d" % z, align_bytes=ALIGN))

        w_halves = [slice(0, N // 2), slice(N // 2, N)]

        def interleave_views(z, cols):
            return (
                w_bf16[z][:, cols, :].rearrange("p (c i) t -> p c t i", i=RUN),
                w_raw[z][:].rearrange("p (t m) -> p t m", t=PACK)[:, :, cols].rearrange("p t (c i) -> p c t i", i=RUN),
            )

        def quantize(z, cols):
            nc.vector.quantize_mx(
                out=w_codes[z][:, cols].bitcast(FP8X4),
                scales=w_plane[z][:, cols],
                in_=w_bf16[z][:, cols, :].rearrange("p m t -> p (m t)"),
            )

        for cols in w_halves:
            nc.vector.tensor_copy(*interleave_views(0, cols))
        for cols in w_halves:
            quantize(0, cols)
        nc.scalar.activation(*interleave_views(1, slice(N - SCALAR_COLS, N)), COPY)
        nc.vector.tensor_copy(*interleave_views(1, slice(N // 2, N - SCALAR_COLS)))
        nc.vector.tensor_copy(*interleave_views(1, w_halves[0]))
        quantize(1, w_halves[1])
        quantize(1, w_halves[0])

        banks = [psum.tile([P, BANK], F32, name="bank%d" % i) for i in range(T // BANK)]
        y = keep.tile([P, T + SPARE], F32, name="y", align_bytes=ALIGN)
        for codes, (z0, z1, a, b) in zip(x_codes, x_pieces):
            for z in range(z0, z1):
                for c in range(a, b, BANK):
                    nc.tensor.matmul_mx(
                        out=banks[c // BANK][:],
                        lhsT=w_codes[z][:].bitcast(FP8X4),
                        lhsT_scale=w_plane[z][:],
                        rhs=codes[:, z - z0, c - a : c - a + BANK].bitcast(FP8X4),
                        rhs_scale=x_plane[:, z, c : c + BANK],
                        start=(z == 0),
                        stop=(z == PASSES - 1),
                    )
                    if z == PASSES - 1:
                        nc.scalar.copy(out=y[:, c : c + BANK], in_=banks[c // BANK][:])

        right_part = keep.tile([P, T], F32, name="right_part", align_bytes=ALIGN)
        left_cols = keep.tile([P, T], F32, name="left_cols", align_bytes=ALIGN)
        left_part = keep.tile([P, T], F32, name="left_part", align_bytes=ALIGN)
        result = keep.tile([P, T], F32, name="result", align_bytes=ALIGN)

        def gather_right(a, b):
            offs = right_offs[:, a // STRIPE : b // STRIPE]
            nc.vector.tensor_tensor(right_part[:, a:b], y[:].indirect(offs), f_right[:, a:b], MULT)

        def gather_left(a, b):
            nc.scalar.activation(left_cols[:, a:b], y[:].indirect(left_offs[:, a // STRIPE : b // STRIPE]), COPY)

        def weigh_left(a, b):
            nc.vector.scalar_tensor_tensor(left_part[:, a:b], f_right[:, a:b], 1.0, left_cols[:, a:b], SUB, MULT)

        def combine(a, b):
            nc.vector.tensor_tensor(result[:, a:b], right_part[:, a:b], left_part[:, a:b], SUB)

        def store(a, b):
            nc.sync.dma_start(out=out[:, a:b], in_=result[:, a:b])

        gather_right(0, T)
        weighed = [(0, 128), (128, 384), (384, T)]
        stored = [(0, 128), (128, 320), (320, T)]
        for cut in weighed:
            gather_left(*cut)
        weigh_left(*weighed[0])
        weigh_left(*weighed[1])
        combine(*stored[0])
        store(*stored[0])
        weigh_left(*weighed[2])
        for cut in stored[1:]:
            combine(*cut)
            store(*cut)
